import numpy as np
import ml_dtypes


def mxq(x, axis, fmt="e4m3"):
    dtype, down = {"e4m3": (ml_dtypes.float8_e4m3fn, 7), "e5m2": (ml_dtypes.float8_e5m2, 14)}[fmt]
    v = np.moveaxis(np.asarray(x, np.float32).astype(ml_dtypes.bfloat16).astype(np.float64), axis, -1)
    blocks = v.reshape(v.shape[:-1] + (-1, 32))
    amax = np.abs(blocks).max(-1, keepdims=True)
    byte = np.maximum(np.where(amax > 0, np.frexp(amax)[1] - 1 + 127, 0) - down, 1)
    scale = np.exp2(byte - 127.0)
    codes = (blocks / scale).astype(np.float32).astype(dtype).astype(np.float64)
    return np.moveaxis((codes * scale).reshape(v.shape), -1, axis)


WIDE = False


def mx_kscale(k):
    if not WIDE:
        return np.ones(k)
    levels = np.array([10, -10, 5, -5, 0])
    if k % 512:
        return np.exp2(np.random.permutation(np.resize(levels, k // 32))).repeat(32)
    a = np.empty((k // 512, 16))
    for p in range(k // 512):
        a[p, :8] = np.random.permutation(np.resize(levels, 8))
        for g in range(8):
            far = levels[np.abs(levels - a[p, g]) >= 10]
            a[p, g + 8] = far[np.random.randint(len(far))]
    return np.exp2(a.ravel()).repeat(32)


def f64(x):
    return np.asarray(x).astype(np.float64)


def striped(idx):
    return np.tile(np.asarray(idx).reshape(-1, 16).T, (8, 1)).astype(np.uint16)


def unstriped(offs):
    return offs[:16].T.reshape(-1).astype(np.int64)


E2M1 = np.array([0.0, 0.5, 1.0, 1.5, 2.0, 3.0, 4.0, 6.0, -0.0, -0.5, -1.0, -1.5, -2.0, -3.0, -4.0, -6.0])


def pack_weight(w, fmt):
    k, n = w.shape
    w = f64(np.asarray(w, np.float32).astype(ml_dtypes.bfloat16)).reshape(k // 32, 32, n)
    amax = np.abs(w).max(1)
    if fmt == "e4m3":
        byte = np.frexp(amax)[1] - 1 + 127 - 7
    else:
        mant, ex = np.frexp(amax / 6.0)
        byte = np.where(mant > 0.5, ex, ex - 1) + 127
    byte = np.clip(np.where(amax > 0, byte, 1), 1, 254)
    scaled = (w * np.exp2(127.0 - byte)[:, None, :]).reshape(k, n).astype(np.float32)
    by_word = np.ascontiguousarray(scaled.reshape(k // 512, 128, 4, n).transpose(0, 1, 3, 2))
    if fmt == "e4m3":
        words = by_word.astype(ml_dtypes.float8_e4m3fn).view(np.uint8)
    else:
        c = by_word.astype(ml_dtypes.float4_e2m1fn).view(np.uint8) & 0xF
        words = (c[..., 0::2] | (c[..., 1::2] << 4)).reshape(k // 512, 128, 2 * n)
    return np.ascontiguousarray(words), np.ascontiguousarray(byte.astype(np.uint8).reshape(k // 512, 16, n))


def unpack_weight(words, scales, fmt):
    g, _, n = scales.shape
    words = np.ascontiguousarray(words).reshape(g, 128, n, -1)
    if fmt == "e4m3":
        vals = words.view(ml_dtypes.float8_e4m3fn).astype(np.float64)
    else:
        nib = np.empty((g, 128, n, 4), np.uint8)
        nib[..., 0::2] = words & 0xF
        nib[..., 1::2] = words >> 4
        vals = E2M1[nib]
    vals = vals * np.repeat(np.exp2(scales.astype(np.float64) - 127.0), 8, axis=1)[..., None]
    return vals.transpose(0, 1, 3, 2).reshape(g * 512, n)


def sigmoid(v):
    return 1.0 / (1.0 + np.exp(-v))


D, E, T, I, Q, G = 512, 512, 2048, 512, 128, 32


def setup_inputs():
    n = np.random.standard_normal
    idx = np.random.permutation(T)[:I]
    fd = mx_kscale(D)
    fe = mx_kscale(E)
    keysp = pack_weight(n((D, T)) / fd[:, None], "e2m1")
    valsp = pack_weight(n((E, T)) / fe[:, None], "e2m1")
    return {
        "query": (n((D, Q)) * 0.5 / np.sqrt(D) * fd[:, None]).astype(np.float32),
        "keys_words": keysp[0],
        "keys_scales": keysp[1],
        "helpf": (np.random.uniform(0.5, 1.5, (Q, 1))).astype(np.float32),
        "gout": (n((E, Q)) * 1 / np.sqrt(E) * fe[:, None]).astype(np.float32),
        "vals_words": valsp[0],
        "vals_scales": valsp[1],
        "dquery": (n((D, Q)) * 1.0 / np.sqrt(D) * fd[:, None]).astype(np.float32),
        "base": (0.5 * n((Q, T))).astype(np.float32),
        "offs": striped(idx),
    }


def reference(query, keys_words, keys_scales, helpf, gout, vals_words, vals_scales, dquery, base, offs):
    idx = unstriped(offs)
    keysu = unpack_weight(keys_words, keys_scales, "e2m1")
    valsu = unpack_weight(vals_words, vals_scales, "e2m1")
    queryq = mxq(f64(query), 0, "e4m3")
    keysidxg = keysu[:, idx]
    a = queryq.T @ keysidxg
    dqueryq = mxq(f64(dquery), 0, "e4m3")
    ta = dqueryq.T @ keysidxg
    m1 = a.reshape(Q, G, I // G).mean(axis=2)
    gt = sigmoid(m1 * 4.0)
    gr = np.repeat(gt, I // G, axis=1)
    s = a * (gr * f64(helpf) + 1.0)
    p = np.exp(s - np.max(s, axis=1, keepdims=True))
    z = np.sum(p, axis=1, keepdims=True)
    goutq = mxq(f64(gout), 0, "e4m3")
    valsidxg = valsu[:, idx]
    c0 = goutq.T @ valsidxg
    dz = np.sum(c0 * p / np.square(z) * (-1.0), axis=1, keepdims=True)
    dp = c0 / z + dz
    ds = dp * p
    dgr = ds * a * f64(helpf)
    dgt = dgr.reshape(Q, G, I // G).sum(axis=2)
    tm1 = ta.reshape(Q, G, I // G).mean(axis=2)
    tgt = tm1 * 4.0 * gt * (1.0 - gt)
    tgr = np.repeat(tgt, I // G, axis=1)
    ts = ta * (gr * f64(helpf) + 1.0) + tgr * f64(helpf) * a
    tp = ts * p
    tz = np.sum(tp, axis=1, keepdims=True)
    tdz = np.sum((tp * c0 - tz * z * 2.0 * c0 * p / np.square(z)) / np.square(z) * (-1.0), axis=1, keepdims=True)
    tdp = tz * c0 / np.square(z) * (-1.0) + tdz
    tds = tdp * p + tp * dp
    tdgr = (tds * a + ta * ds) * f64(helpf)
    tdgt = tdgr.reshape(Q, G, I // G).sum(axis=2)
    tdm1 = ((tdgt * gt + tgt * dgt) * (1.0 - gt) + tgt * (-1.0) * dgt * gt) * 4.0
    te1 = tdm1 / 16.0
    tr1 = np.repeat(te1, I // G, axis=1)
    tda = tds * (gr * f64(helpf) + 1.0) + tgr * f64(helpf) * ds + tr1
    gs = tda * 512.0
    gf = np.zeros((Q, T))
    gf[:, idx] = gs
    y = f64(base) + gf
    return y

@@ -1,0 +1,231 @@
+from contextlib import ExitStack
+
+import concourse.mybir as mybir
+
+D, E, T, I, Q, G = 512, 512, 2048, 512, 128, 32
+PAGE = I // G
+FLOPS = 3 * 2 * D * Q * I
+
+F32 = mybir.dt.float32
+BF16 = mybir.dt.bfloat16
+I32 = mybir.dt.int32
+U32 = mybir.dt.uint32
+U16 = mybir.dt.uint16
+U8 = mybir.dt.uint8
+FP8X4 = mybir.dt.float8_e4m3fn_x4
+FP4X4 = mybir.dt.float4_e2m1fn_x4
+ALU = mybir.AluOpType
+ACT = mybir.ActivationFunctionType
+AX = mybir.AxisListType
+
+P = 128
+PACK = 4
+HALF = I // 2
+STORE_WIDTHS = (256, 512, 512, 512, 256)
+
+
+def tile_attend_hvpagemates_s_kernel(tc, query, keys_words, keys_scales, helpf, gout, vals_words, vals_scales, dquery, base, offs, out):
+    nc = tc.nc
+    with ExitStack() as ctx:
+        sb = ctx.enter_context(tc.tile_pool(name="sb", bufs=1))
+        psum = ctx.enter_context(tc.psum_pool(name="psum", bufs=1))
+
+        def wide(name):
+            return sb.tile([P, I], F32, name=name)
+
+        def narrow(name, columns=G):
+            return sb.tile([P, columns], F32, name=name)
+
+        def paged(ap):
+            return ap.rearrange("p (g j) -> p g j", j=PAGE)
+
+        def spread(ap):
+            return ap.unsqueeze(2).to_broadcast([P, ap.shape[1], PAGE])
+
+        offsets = sb.tile([P, I // 16], U16, name="offsets")
+        nc.sync.dma_start(offsets[:], offs)
+
+        def load_words(name, tag, words):
+            pool_words = sb.tile([P, T], U16, name=name, tag=tag)
+            nc.sync.dma_start(out=pool_words[:].bitcast(I32), in_=words[0].bitcast(I32))
+            return pool_words
+
+        def load_scales(name, scales, queue):
+            pool_scales = sb.tile([P, T], U8, name=name)
+            nc.vector.memset(pool_scales[:].bitcast(I32), 0)
+            for quadrant in range(4):
+                queue.dma_start(
+                    out=pool_scales[32 * quadrant : 32 * quadrant + 4, :].bitcast(I32),
+                    in_=scales[0, 4 * quadrant : 4 * quadrant + 4, :].bitcast(I32),
+                )
+            return pool_scales
+
+        def load_rows(name, tag, rows):
+            raw = sb.tile([P, PACK, Q], F32, name=name, tag=tag)
+            nc.sync.dma_start(out=raw[:], in_=rows.rearrange("(p t) q -> p t q", t=PACK))
+            return raw
+
+        def interleave(name, raw):
+            grouped = sb.tile([P, Q, PACK], BF16, name=name, align_bytes=64)
+            nc.scalar.copy(
+                out=grouped[:].rearrange("p (c i) t -> p c t i", i=4),
+                in_=raw[:].rearrange("p t (c i) -> p c t i", i=4),
+            )
+            return grouped
+
+        def quantize(name, grouped):
+            codes = sb.tile([P, Q], U32, name=name + "_codes", align_bytes=64)
+            scales = sb.tile([P, Q], U8, name=name + "_scales", align_bytes=64)
+            nc.vector.quantize_mx(out=codes[:].bitcast(FP8X4), scales=scales[:], in_=grouped[:].rearrange("p q t -> p (q t)"))
+            return codes, scales
+
+        def gather(name, window, dtype):
+            picked = sb.tile([P, I], dtype, name=name, align_bytes=64)
+            nc.vector.tensor_copy(out=picked[:], in_=window[:].indirect(offsets[:]))
+            return picked
+
+        def product(name, rows, words, scales):
+            bank = psum.tile([P, I], F32, name=name)
+            nc.tensor.matmul_mx(out=bank[:], lhsT=rows[0][:].bitcast(FP8X4), lhsT_scale=rows[1][:],
+                                rhs=words[:].bitcast(FP4X4), rhs_scale=scales[:], start=True, stop=True)
+            return bank
+
+        def by_page(dst, src, pages, scale, bias=None):
+            for g in pages:
+                columns = slice(g * PAGE, (g + 1) * PAGE)
+                if bias is None:
+                    nc.scalar.activation(out=dst[:, columns], in_=src[:, columns], func=ACT.Copy, scale=scale[:, g : g + 1])
+                else:
+                    nc.scalar.activation(out=dst[:, columns], in_=src[:, columns], func=ACT.Identity, scale=scale[:, g : g + 1], bias=bias[:, g : g + 1])
+
+        keys_pool = load_words("keys_pool", "keys_then_base", keys_words)
+        keys_plane = load_scales("keys_plane", keys_scales, nc.scalar)
+        query_raw = load_rows("query_raw", "query_then_gout", query)
+        dquery_raw = load_rows("dquery_raw", "dquery_raw", dquery)
+        warm = narrow("warm", 2)
+        nc.vector.memset(warm[:, 0:1], 0.0)
+        nc.scalar.activation(out=warm[:, 1:2], in_=warm[:, 0:1], func=ACT.Exp)
+        vals_pool = load_words("vals_pool", "vals_pool", vals_words)
+        vals_plane = load_scales("vals_plane", vals_scales, nc.sync)
+        help_col = narrow("help_col", 1)
+        nc.sync.dma_start(out=help_col[:], in_=helpf)
+        window = sb.tile([P, T], F32, name="window")
+        nc.vector.memset(window[:], 0.0)
+
+        hc = narrow("hc", 4)
+        for column, (factor, shift) in enumerate(((0.5, 0.0), (0.5, 1.0), (-1.0 / 16, 0.0), (1.0 / 16, 0.0))):
+            nc.gpsimd.tensor_scalar(out=hc[:, column : column + 1], in0=help_col[:], scalar1=factor, scalar2=shift, op0=ALU.mult, op1=ALU.add)
+
+        query_bf = interleave("query_bf", query_raw)
+        dquery_bf = interleave("dquery_bf", dquery_raw)
+        gout_raw = load_rows("gout_raw", "query_then_gout", gout)
+        gout_bf = interleave("gout_bf", gout_raw)
+        keys_w = gather("keys_w", keys_pool, U16)
+        base_sb = sb.tile([P, T], F32, name="base_sb", tag="keys_then_base")
+        nc.sync.dma_start(out=base_sb[:], in_=base)
+        keys_s = gather("keys_s", keys_plane, U8)
+        a = product("a", quantize("query", query_bf), keys_w, keys_s)
+        ta = product("ta", quantize("dquery", dquery_bf), keys_w, keys_s)
+        vals_s = gather("vals_s", vals_plane, U8)
+
+        a_sum = narrow("a_sum")
+        nc.vector.tensor_reduce(out=a_sum[:], in_=paged(a[:]), axis=AX.X, op=ALU.add)
+        ta_sum = narrow("ta_sum")
+        nc.vector.tensor_reduce(out=ta_sum[:], in_=paged(ta[:]), axis=AX.X, op=ALU.add)
+        th = narrow("th")
+        nc.scalar.activation(out=th[:], in_=a_sum[:], func=ACT.Tanh, scale=0.125)
+        fac = narrow("fac")
+        nc.scalar.activation(out=fac[:], in_=th[:], func=ACT.Identity, scale=hc[:, 0:1], bias=hc[:, 1:2])
+        th2 = narrow("th2")
+        nc.scalar.activation(out=th2[:], in_=th[:], func=ACT.Square)
+        kt = sb.tile([P, 2, G], F32, name="kt")
+        nc.scalar.activation(out=kt[:, 1, :], in_=th[:], func=ACT.Copy, scale=0.25)
+        nc.scalar.activation(out=kt[:, 0, :], in_=th2[:], func=ACT.Identity, scale=hc[:, 2:3], bias=hc[:, 3:4])
+        a_sb = wide("a_sb")
+        nc.scalar.copy(out=a_sb[:], in_=a[:])
+        gout_q = quantize("gout", gout_bf)
+        uk = sb.tile([P, 2, G], F32, name="uk")
+        nc.vector.tensor_tensor(out=uk[:], in0=kt[:], in1=ta_sum[:].unsqueeze(1).to_broadcast([P, 2, G]), op=ALU.mult)
+        vals_w = gather("vals_w", vals_pool, U16)
+        c = product("c", gout_q, vals_w, vals_s)
+
+        ua = wide("ua")
+        by_page(ua, a_sb, range(G), uk[:, 0, :])
+        s = wide("s")
+        nc.vector.tensor_tensor(out=paged(s[:]), in0=paged(a[:]), in1=spread(fac[:]), op=ALU.mult)
+        taf = wide("taf")
+        nc.vector.tensor_tensor(out=paged(taf[:]), in0=paged(ta[:]), in1=spread(fac[:]), op=ALU.mult)
+        st = narrow("st", 8)
+        negmax, z, rz, cbar, tbar, cov = (st[:, j : j + 1] for j in range(6))
+        nc.vector.tensor_reduce(out=negmax, in_=s[:], axis=AX.X, op=ALU.max, negate=True)
+        e = wide("e")
+        nc.scalar.activation(out=e[:], in_=s[:], func=ACT.Exp, bias=negmax, accum_out=z)
+        ka = wide("ka")
+        nc.vector.tensor_tensor(out=paged(ka[:]), in0=paged(a[:]), in1=spread(uk[:, 1, :]), op=ALU.mult)
+        ts = wide("ts")
+        nc.vector.tensor_tensor(out=ts[:], in0=taf[:], in1=ua[:], op=ALU.add)
+        nc.vector.reciprocal(out=rz, in_=z)
+        prob = wide("prob")
+        nc.scalar.activation(out=prob[:], in_=e[:], func=ACT.Copy, scale=rz)
+        nfac512 = narrow("nfac512")
+        nc.scalar.activation(out=nfac512[:], in_=fac[:], func=ACT.Copy, scale=-512.0)
+        u512 = narrow("u512")
+        nc.scalar.activation(out=u512[:], in_=uk[:, 0, :], func=ACT.Copy, scale=512.0)
+
+        pc = wide("pc")
+        nc.vector.scalar_tensor_tensor(out=pc[:], in0=c[:], scalar=rz, in1=e[:], op0=ALU.mult, op1=ALU.mult, accum_out=cbar)
+        pts = wide("pts")
+        nc.vector.scalar_tensor_tensor(out=pts[:], in0=ts[:], scalar=rz, in1=e[:], op0=ALU.mult, op1=ALU.mult, accum_out=tbar)
+        ds = wide("ds")
+        nc.vector.scalar_tensor_tensor(out=ds[:], in0=c[:], scalar=cbar, in1=prob[:], op0=ALU.subtract, op1=ALU.mult)
+        nv = wide("nv")
+        nc.vector.tensor_tensor(out=nv[:], in0=ka[:], in1=ta[:], op=ALU.subtract)
+        r = wide("r")
+        nc.vector.scalar_tensor_tensor(out=r[:], in0=ts[:], scalar=tbar, in1=ds[:], op0=ALU.subtract, op1=ALU.mult, accum_out=cov)
+        du = wide("du")
+        by_page(du, ds, range(G), u512)
+
+        terms = sb.tile([P, 2, I], F32, name="terms")
+        ntds = wide("ntds")
+        nx = narrow("nx")
+        te = narrow("te")
+        zed = wide("zed")
+        halves = [slice(h * HALF, (h + 1) * HALF) for h in range(2)]
+        half_pages = [slice(h * G // 2, (h + 1) * G // 2) for h in range(2)]
+
+        def ds_nv(h):
+            nc.vector.tensor_tensor(out=terms[:, 1, halves[h]], in0=ds[:, halves[h]], in1=nv[:, halves[h]], op=ALU.mult)
+
+        def make_ntds(h):
+            nc.vector.scalar_tensor_tensor(out=ntds[:, halves[h]], in0=prob[:, halves[h]], scalar=cov, in1=r[:, halves[h]], op0=ALU.mult, op1=ALU.subtract)
+
+        def ntds_a(h):
+            nc.vector.tensor_tensor(out=terms[:, 0, halves[h]], in0=a[:, halves[h]], in1=ntds[:, halves[h]], op=ALU.mult)
+
+        def page_sums(h):
+            nc.vector.tensor_reduce(out=nx[:, half_pages[h]], in_=terms[:, :, halves[h]].rearrange("p s (g j) -> p g s j", j=PAGE), axis=AX.XY, op=ALU.add)
+
+        def make_te(h):
+            nc.vector.scalar_tensor_tensor(out=te[:, half_pages[h]], in0=nx[:, half_pages[h]], scalar=-512.0, in1=kt[:, 0, half_pages[h]], op0=ALU.mult, op1=ALU.mult)
+            by_page(zed, ntds, range(half_pages[h].start, half_pages[h].stop), nfac512, te)
+
+        ds_nv(0)
+        make_ntds(0)
+        make_ntds(1)
+        ntds_a(0)
+        ds_nv(1)
+        page_sums(0)
+        ntds_a(1)
+        make_te(0)
+        page_sums(1)
+        make_te(1)
+        for h in range(2):
+            nc.vector.tensor_tensor(out=window[:].indirect(offsets[:, half_pages[h]]), in0=zed[:, halves[h]], in1=du[:, halves[h]], op=ALU.add)
+
+        start = 0
+        for index, width in enumerate(STORE_WIDTHS):
+            columns = slice(start, start + width)
+            result = sb.tile([P, width], F32, name="result%d" % index)
+            nc.vector.tensor_tensor(out=result[:], in0=base_sb[:, columns], in1=window[:, columns], op=ALU.add)
+            nc.sync.dma_start(out=out[:, columns], in_=result[:])
+            start = start + width

@@ -65,8 +65,8 @@ def tile_attend_hvpagemates_s_kernel(tc, query, keys_words, keys_scales, helpf, 
             nc.sync.dma_start(out=raw[:], in_=rows.rearrange("(p t) q -> p t q", t=PACK))
             return raw
 
-        def interleave(name, raw):
-            grouped = sb.tile([P, Q, PACK], BF16, name=name, align_bytes=64)
+        def interleave(name, tag, raw):
+            grouped = sb.tile([P, Q, PACK], BF16, name=name, tag=tag, align_bytes=64)
             nc.scalar.copy(
                 out=grouped[:].rearrange("p (c i) t -> p c t i", i=4),
                 in_=raw[:].rearrange("p t (c i) -> p c t i", i=4),
@@ -79,36 +79,33 @@ def tile_attend_hvpagemates_s_kernel(tc, query, keys_words, keys_scales, helpf, 
             nc.vector.quantize_mx(out=codes[:].bitcast(FP8X4), scales=scales[:], in_=grouped[:].rearrange("p q t -> p (q t)"))
             return codes, scales
 
-        def gather(name, window, dtype):
-            picked = sb.tile([P, I], dtype, name=name, align_bytes=64)
-            nc.vector.tensor_copy(out=picked[:], in_=window[:].indirect(offsets[:]))
-            return picked
+        halves = [slice(h * HALF, (h + 1) * HALF) for h in range(2)]
+        half_pages = [slice(h * G // 2, (h + 1) * G // 2) for h in range(2)]
 
-        def product(name, rows, words, scales):
-            bank = psum.tile([P, I], F32, name=name)
-            nc.tensor.matmul_mx(out=bank[:], lhsT=rows[0][:].bitcast(FP8X4), lhsT_scale=rows[1][:],
-                                rhs=words[:].bitcast(FP4X4), rhs_scale=scales[:], start=True, stop=True)
-            return bank
+        def gather(picked, window, pages):
+            nc.vector.tensor_copy(out=picked[:], in_=window[:].indirect(offsets[:, pages]))
 
-        def by_page(dst, src, pages, scale, bias=None):
-            for g in pages:
+        def product(dst, rows, words, scales):
+            nc.tensor.matmul_mx(out=dst, lhsT=rows[0][:].bitcast(FP8X4), lhsT_scale=rows[1][:],
+                                rhs=words.bitcast(FP4X4), rhs_scale=scales, start=True, stop=True)
+
+        def by_page(dst, src, scale):
+            for g in range(scale.shape[1]):
                 columns = slice(g * PAGE, (g + 1) * PAGE)
-                if bias is None:
-                    nc.scalar.activation(out=dst[:, columns], in_=src[:, columns], func=ACT.Copy, scale=scale[:, g : g + 1])
-                else:
-                    nc.scalar.activation(out=dst[:, columns], in_=src[:, columns], func=ACT.Identity, scale=scale[:, g : g + 1], bias=bias[:, g : g + 1])
+                nc.scalar.activation(out=dst[:, columns], in_=src[:, columns], func=ACT.Copy, scale=scale[:, g : g + 1])
 
+        all_pages = slice(0, G)
         keys_pool = load_words("keys_pool", "keys_then_base", keys_words)
         keys_plane = load_scales("keys_plane", keys_scales, nc.scalar)
         query_raw = load_rows("query_raw", "query_then_gout", query)
         dquery_raw = load_rows("dquery_raw", "dquery_raw", dquery)
-        warm = narrow("warm", 2)
+        warm = sb.tile([P, 2], F32, name="warm", tag="warm_then_vals")
         nc.vector.memset(warm[:, 0:1], 0.0)
         nc.scalar.activation(out=warm[:, 1:2], in_=warm[:, 0:1], func=ACT.Exp)
-        vals_pool = load_words("vals_pool", "vals_pool", vals_words)
         vals_plane = load_scales("vals_plane", vals_scales, nc.sync)
+        vals_pool = load_words("vals_pool", "warm_then_vals", vals_words)
         help_col = narrow("help_col", 1)
-        nc.sync.dma_start(out=help_col[:], in_=helpf)
+        nc.gpsimd.dma_start(out=help_col[:], in_=helpf)
         window = sb.tile([P, T], F32, name="window")
         nc.vector.memset(window[:], 0.0)
 
@@ -116,111 +113,113 @@ def tile_attend_hvpagemates_s_kernel(tc, query, keys_words, keys_scales, helpf, 
         for column, (factor, shift) in enumerate(((0.5, 0.0), (0.5, 1.0), (-1.0 / 16, 0.0), (1.0 / 16, 0.0))):
             nc.gpsimd.tensor_scalar(out=hc[:, column : column + 1], in0=help_col[:], scalar1=factor, scalar2=shift, op0=ALU.mult, op1=ALU.add)
 
-        query_bf = interleave("query_bf", query_raw)
-        dquery_bf = interleave("dquery_bf", dquery_raw)
+        query_bf = interleave("query_bf", "query_bf_then_keys_s1", query_raw)
+        dquery_bf = interleave("dquery_bf", "dquery_bf", dquery_raw)
         gout_raw = load_rows("gout_raw", "query_then_gout", gout)
-        gout_bf = interleave("gout_bf", gout_raw)
-        keys_w = gather("keys_w", keys_pool, U16)
+        keys_w = sb.tile([P, I], U16, name="keys_w", align_bytes=64)
+        keys_s = [sb.tile([P, HALF], U8, name="keys_s0", align_bytes=64)]
+        gather(keys_w, keys_pool, all_pages)
         base_sb = sb.tile([P, T], F32, name="base_sb", tag="keys_then_base")
         nc.sync.dma_start(out=base_sb[:], in_=base)
-        keys_s = gather("keys_s", keys_plane, U8)
-        a = product("a", quantize("query", query_bf), keys_w, keys_s)
-        ta = product("ta", quantize("dquery", dquery_bf), keys_w, keys_s)
-        vals_s = gather("vals_s", vals_plane, U8)
-
-        a_sum = narrow("a_sum")
-        nc.vector.tensor_reduce(out=a_sum[:], in_=paged(a[:]), axis=AX.X, op=ALU.add)
-        ta_sum = narrow("ta_sum")
-        nc.vector.tensor_reduce(out=ta_sum[:], in_=paged(ta[:]), axis=AX.X, op=ALU.add)
+        gather(keys_s[0], keys_plane, half_pages[0])
+        query_q = quantize("query", query_bf)
+        keys_s.append(sb.tile([P, HALF], U8, name="keys_s1", tag="query_bf_then_keys_s1", align_bytes=64))
+        gather(keys_s[1], keys_plane, half_pages[1])
+        a = [psum.tile([P, I], F32, name="a%d" % h)[:, 0:HALF] for h in range(2)]
+        for h in range(2):
+            product(a[h], query_q, keys_w[:, halves[h]], keys_s[h][:])
+        a_sum = sb.tile([P, G], F32, name="a_sum")
+        nc.vector.tensor_reduce(out=a_sum[:, half_pages[0]], in_=paged(a[0]), axis=AX.X, op=ALU.add)
+        dquery_q = quantize("dquery", dquery_bf)
+        ta = psum.tile([P, I], F32, name="ta")[:]
+        for h in range(2):
+            product(ta[:, halves[h]], dquery_q, keys_w[:, halves[h]], keys_s[h][:])
+        a_sb = wide("a_sb")
+        nc.scalar.copy(out=a_sb[:, halves[0]], in_=a[0])
+        nc.vector.tensor_reduce(out=a_sum[:, half_pages[1]], in_=paged(a[1]), axis=AX.X, op=ALU.add)
         th = narrow("th")
         nc.scalar.activation(out=th[:], in_=a_sum[:], func=ACT.Tanh, scale=0.125)
         fac = narrow("fac")
         nc.scalar.activation(out=fac[:], in_=th[:], func=ACT.Identity, scale=hc[:, 0:1], bias=hc[:, 1:2])
+        ta_sb = wide("ta_sb")
+        nc.scalar.copy(out=ta_sb[:], in_=ta)
+        taf = wide("taf")
+        nc.gpsimd.tensor_tensor(out=paged(taf[:]), in0=paged(ta_sb[:]), in1=spread(fac[:]), op=ALU.mult)
         th2 = narrow("th2")
         nc.scalar.activation(out=th2[:], in_=th[:], func=ACT.Square)
         kt = sb.tile([P, 2, G], F32, name="kt")
         nc.scalar.activation(out=kt[:, 1, :], in_=th[:], func=ACT.Copy, scale=0.25)
         nc.scalar.activation(out=kt[:, 0, :], in_=th2[:], func=ACT.Identity, scale=hc[:, 2:3], bias=hc[:, 3:4])
-        a_sb = wide("a_sb")
-        nc.scalar.copy(out=a_sb[:], in_=a[:])
-        gout_q = quantize("gout", gout_bf)
+        nc.scalar.copy(out=a_sb[:, halves[1]], in_=a[1])
+        gout_bf = interleave("gout_bf", "gout_bf", gout_raw)
+        vals_s = sb.tile([P, I], U8, name="vals_s", align_bytes=64)
+        gather(vals_s, vals_plane, all_pages)
+        ta_sum = sb.tile([P, G], F32, name="ta_sum", tag="ta_sum_then_vals_w", align_bytes=64)
+        nc.vector.tensor_reduce(out=ta_sum[:], in_=paged(ta), axis=AX.X, op=ALU.add)
+        s = sb.tile([P, I], F32, name="s", tag="s_then_ka1")
+        for h in range(2):
+            nc.vector.tensor_tensor(out=paged(s[:, halves[h]]), in0=paged(a[h]), in1=spread(fac[:, half_pages[h]]), op=ALU.mult)
         uk = sb.tile([P, 2, G], F32, name="uk")
         nc.vector.tensor_tensor(out=uk[:], in0=kt[:], in1=ta_sum[:].unsqueeze(1).to_broadcast([P, 2, G]), op=ALU.mult)
-        vals_w = gather("vals_w", vals_pool, U16)
-        c = product("c", gout_q, vals_w, vals_s)
-
-        ua = wide("ua")
-        by_page(ua, a_sb, range(G), uk[:, 0, :])
-        s = wide("s")
-        nc.vector.tensor_tensor(out=paged(s[:]), in0=paged(a[:]), in1=spread(fac[:]), op=ALU.mult)
-        taf = wide("taf")
-        nc.vector.tensor_tensor(out=paged(taf[:]), in0=paged(ta[:]), in1=spread(fac[:]), op=ALU.mult)
+        ua = sb.tile([P, I], F32, name="ua", tag="ua_then_nv")
+        nc.gpsimd.tensor_tensor(out=paged(ua[:]), in0=paged(a_sb[:]), in1=spread(uk[:, 0, :]), op=ALU.mult)
         st = narrow("st", 8)
         negmax, z, rz, cbar, tbar, cov = (st[:, j : j + 1] for j in range(6))
         nc.vector.tensor_reduce(out=negmax, in_=s[:], axis=AX.X, op=ALU.max, negate=True)
         e = wide("e")
         nc.scalar.activation(out=e[:], in_=s[:], func=ACT.Exp, bias=negmax, accum_out=z)
-        ka = wide("ka")
-        nc.vector.tensor_tensor(out=paged(ka[:]), in0=paged(a[:]), in1=spread(uk[:, 1, :]), op=ALU.mult)
-        ts = wide("ts")
-        nc.vector.tensor_tensor(out=ts[:], in0=taf[:], in1=ua[:], op=ALU.add)
+        gout_q = quantize("gout", gout_bf)
+        vals_w = sb.tile([P, I], U16, name="vals_w", tag="ta_sum_then_vals_w", align_bytes=64)
+        gather(vals_w, vals_pool, all_pages)
+        c = psum.tile([P, I], F32, name="c")[:]
+        product(c, gout_q, vals_w[:], vals_s[:])
         nc.vector.reciprocal(out=rz, in_=z)
         prob = wide("prob")
         nc.scalar.activation(out=prob[:], in_=e[:], func=ACT.Copy, scale=rz)
+        ts = wide("ts")
+        nc.vector.tensor_tensor(out=ts[:], in0=taf[:], in1=ua[:], op=ALU.add)
+        ka = [narrow("ka0", HALF), sb.tile([P, HALF], F32, name="ka1", tag="s_then_ka1")]
+        for h in range(2):
+            by_page(ka[h], a_sb[:, halves[h]], uk[:, 1, half_pages[h]])
         nfac512 = narrow("nfac512")
         nc.scalar.activation(out=nfac512[:], in_=fac[:], func=ACT.Copy, scale=-512.0)
         u512 = narrow("u512")
         nc.scalar.activation(out=u512[:], in_=uk[:, 0, :], func=ACT.Copy, scale=512.0)
 
-        pc = wide("pc")
-        nc.vector.scalar_tensor_tensor(out=pc[:], in0=c[:], scalar=rz, in1=e[:], op0=ALU.mult, op1=ALU.mult, accum_out=cbar)
         pts = wide("pts")
         nc.vector.scalar_tensor_tensor(out=pts[:], in0=ts[:], scalar=rz, in1=e[:], op0=ALU.mult, op1=ALU.mult, accum_out=tbar)
-        ds = wide("ds")
-        nc.vector.scalar_tensor_tensor(out=ds[:], in0=c[:], scalar=cbar, in1=prob[:], op0=ALU.subtract, op1=ALU.mult)
-        nv = wide("nv")
-        nc.vector.tensor_tensor(out=nv[:], in0=ka[:], in1=ta[:], op=ALU.subtract)
-        r = wide("r")
-        nc.vector.scalar_tensor_tensor(out=r[:], in0=ts[:], scalar=tbar, in1=ds[:], op0=ALU.subtract, op1=ALU.mult, accum_out=cov)
-        du = wide("du")
-        by_page(du, ds, range(G), u512)
-
-        terms = sb.tile([P, 2, I], F32, name="terms")
-        ntds = wide("ntds")
-        nx = narrow("nx")
-        te = narrow("te")
-        zed = wide("zed")
-        halves = [slice(h * HALF, (h + 1) * HALF) for h in range(2)]
-        half_pages = [slice(h * G // 2, (h + 1) * G // 2) for h in range(2)]
-
-        def ds_nv(h):
-            nc.vector.tensor_tensor(out=terms[:, 1, halves[h]], in0=ds[:, halves[h]], in1=nv[:, halves[h]], op=ALU.mult)
-
-        def make_ntds(h):
-            nc.vector.scalar_tensor_tensor(out=ntds[:, halves[h]], in0=prob[:, halves[h]], scalar=cov, in1=r[:, halves[h]], op0=ALU.mult, op1=ALU.subtract)
-
-        def ntds_a(h):
-            nc.vector.tensor_tensor(out=terms[:, 0, halves[h]], in0=a[:, halves[h]], in1=ntds[:, halves[h]], op=ALU.mult)
-
-        def page_sums(h):
-            nc.vector.tensor_reduce(out=nx[:, half_pages[h]], in_=terms[:, :, halves[h]].rearrange("p s (g j) -> p g s j", j=PAGE), axis=AX.XY, op=ALU.add)
-
-        def make_te(h):
-            nc.vector.scalar_tensor_tensor(out=te[:, half_pages[h]], in0=nx[:, half_pages[h]], scalar=-512.0, in1=kt[:, 0, half_pages[h]], op0=ALU.mult, op1=ALU.mult)
-            by_page(zed, ntds, range(half_pages[h].start, half_pages[h].stop), nfac512, te)
-
-        ds_nv(0)
-        make_ntds(0)
-        make_ntds(1)
-        ntds_a(0)
-        ds_nv(1)
-        page_sums(0)
-        ntds_a(1)
-        make_te(0)
-        page_sums(1)
-        make_te(1)
+        nv = sb.tile([P, I], F32, name="nv", tag="ua_then_nv")
         for h in range(2):
-            nc.vector.tensor_tensor(out=window[:].indirect(offsets[:, half_pages[h]]), in0=zed[:, halves[h]], in1=du[:, halves[h]], op=ALU.add)
+            nc.gpsimd.tensor_tensor(out=nv[:, halves[h]], in0=ka[h][:], in1=ta_sb[:, halves[h]], op=ALU.subtract)
+        pc = wide("pc")
+        nc.vector.scalar_tensor_tensor(out=pc[:], in0=c, scalar=rz, in1=e[:], op0=ALU.mult, op1=ALU.mult, accum_out=cbar)
+        ds = wide("ds")
+        nc.vector.scalar_tensor_tensor(out=ds[:], in0=c, scalar=cbar, in1=prob[:], op0=ALU.subtract, op1=ALU.mult)
+        du = wide("du")
+        by_page(du, ds, u512)
+        r = sb.tile([P, I], F32, name="r", tag="r_then_terms1")
+        nc.vector.scalar_tensor_tensor(out=r[:], in0=ts[:], scalar=tbar, in1=ds[:], op0=ALU.subtract, op1=ALU.mult, accum_out=cov)
+        terms = [sb.tile([P, 2, HALF], F32, name="terms0")]
+        nc.vector.tensor_tensor(out=terms[0][:, 1, :], in0=ds[:, halves[0]], in1=nv[:, halves[0]], op=ALU.mult)
+        ntds = wide("ntds")
+        for h in range(2):
+            nc.vector.scalar_tensor_tensor(out=ntds[:, halves[h]], in0=prob[:, halves[h]], scalar=cov, in1=r[:, halves[h]], op0=ALU.mult, op1=ALU.subtract)
+        terms.append(sb.tile([P, 2, HALF], F32, name="terms1", tag="r_then_terms1"))
+        nc.gpsimd.tensor_tensor(out=terms[1][:, 1, :], in0=ds[:, halves[1]], in1=nv[:, halves[1]], op=ALU.mult)
+        yf = wide("yf")
+        by_page(yf, ntds, nfac512)
+        for h in range(2):
+            nc.vector.tensor_tensor(out=terms[h][:, 0, :], in0=a[h], in1=ntds[:, halves[h]], op=ALU.mult)
+        nx = narrow("nx")
+        for h in range(2):
+            nc.vector.tensor_reduce(out=nx[:, half_pages[h]], in_=terms[h][:].rearrange("p s (g j) -> p g s j", j=PAGE), axis=AX.XY, op=ALU.add)
+        te = narrow("te")
+        for h in range(2):
+            nc.vector.scalar_tensor_tensor(out=te[:, half_pages[h]], in0=nx[:, half_pages[h]], scalar=-512.0, in1=kt[:, 0, half_pages[h]], op0=ALU.mult, op1=ALU.mult)
+        y = wide("y")
+        for h in range(2):
+            nc.vector.tensor_tensor(out=paged(y[:, halves[h]]), in0=paged(du[:, halves[h]]), in1=spread(te[:, half_pages[h]]), op=ALU.add)
+        nc.vector.tensor_tensor(out=window[:].indirect(offsets[:]), in0=y[:], in1=yf[:], op=ALU.add)
 
         start = 0
         for index, width in enumerate(STORE_WIDTHS):

@@ -4,7 +4,7 @@ import concourse.mybir as mybir
 
 D, E, T, I, Q, G = 512, 512, 2048, 512, 128, 32
 PAGE = I // G
-FLOPS = 3 * 2 * D * Q * I
+FLOPS = 2 * Q * I * (2 * D + E)
 
 F32 = mybir.dt.float32
 BF16 = mybir.dt.bfloat16
@@ -20,20 +20,27 @@ AX = mybir.AxisListType
 
 P = 128
 PACK = 4
+QUADRANT = 32
+SCALE_ROWS = 4
+LIST_ROWS = 16
 HALF = I // 2
+GS_FACTOR = 512.0
 STORE_WIDTHS = (256, 512, 512, 512, 256)
 
 
-def tile_attend_hvpagemates_s_kernel(tc, query, keys_words, keys_scales, helpf, gout, vals_words, vals_scales, dquery, base, offs, out):
+def tile_attend_hvpagemates_s_kernel(
+    tc, query, keys_words, keys_scales, helpf, gout, vals_words, vals_scales, dquery, base, offs, out
+):
     nc = tc.nc
     with ExitStack() as ctx:
         sb = ctx.enter_context(tc.tile_pool(name="sb", bufs=1))
         psum = ctx.enter_context(tc.psum_pool(name="psum", bufs=1))
 
-        def wide(name):
-            return sb.tile([P, I], F32, name=name)
+        all_pages = slice(0, G)
+        halves = [slice(h * HALF, (h + 1) * HALF) for h in range(2)]
+        half_pages = [slice(h * G // 2, (h + 1) * G // 2) for h in range(2)]
 
-        def narrow(name, columns=G):
+        def floats(name, columns):
             return sb.tile([P, columns], F32, name=name)
 
         def paged(ap):
@@ -41,9 +48,6 @@ def tile_attend_hvpagemates_s_kernel(tc, query, keys_words, keys_scales, helpf, 
 
         def spread(ap):
             return ap.unsqueeze(2).to_broadcast([P, ap.shape[1], PAGE])
-
-        offsets = sb.tile([P, I // 16], U16, name="offsets")
-        nc.sync.dma_start(offsets[:], offs)
 
         def load_words(name, tag, words):
             pool_words = sb.tile([P, T], U16, name=name, tag=tag)
@@ -53,74 +57,86 @@ def tile_attend_hvpagemates_s_kernel(tc, query, keys_words, keys_scales, helpf, 
         def load_scales(name, scales, queue):
             pool_scales = sb.tile([P, T], U8, name=name)
             nc.vector.memset(pool_scales[:].bitcast(I32), 0)
-            for quadrant in range(4):
+            for quadrant in range(P // QUADRANT):
                 queue.dma_start(
-                    out=pool_scales[32 * quadrant : 32 * quadrant + 4, :].bitcast(I32),
-                    in_=scales[0, 4 * quadrant : 4 * quadrant + 4, :].bitcast(I32),
+                    out=pool_scales[QUADRANT * quadrant : QUADRANT * quadrant + SCALE_ROWS, :].bitcast(I32),
+                    in_=scales[0, SCALE_ROWS * quadrant : SCALE_ROWS * (quadrant + 1), :].bitcast(I32),
                 )
             return pool_scales
 
         def load_rows(name, tag, rows):
             raw = sb.tile([P, PACK, Q], F32, name=name, tag=tag)
-            nc.sync.dma_start(out=raw[:], in_=rows.rearrange("(p t) q -> p t q", t=PACK))
+            nc.sync.dma_start(out=raw[:], in_=rows.rearrange("(p r) q -> p r q", r=PACK))
             return raw
 
         def interleave(name, tag, raw):
             grouped = sb.tile([P, Q, PACK], BF16, name=name, tag=tag, align_bytes=64)
-            nc.scalar.copy(
-                out=grouped[:].rearrange("p (c i) t -> p c t i", i=4),
-                in_=raw[:].rearrange("p t (c i) -> p c t i", i=4),
+            nc.scalar.activation(
+                out=grouped[:].rearrange("p (c i) r -> p c r i", i=4),
+                in_=raw[:].rearrange("p r (c i) -> p c r i", i=4),
+                func=ACT.Copy,
             )
             return grouped
 
         def quantize(name, grouped):
             codes = sb.tile([P, Q], U32, name=name + "_codes", align_bytes=64)
             scales = sb.tile([P, Q], U8, name=name + "_scales", align_bytes=64)
-            nc.vector.quantize_mx(out=codes[:].bitcast(FP8X4), scales=scales[:], in_=grouped[:].rearrange("p q t -> p (q t)"))
+            nc.vector.quantize_mx(
+                out=codes[:].bitcast(FP8X4), scales=scales[:], in_=grouped[:].rearrange("p q r -> p (q r)")
+            )
             return codes, scales
 
-        halves = [slice(h * HALF, (h + 1) * HALF) for h in range(2)]
-        half_pages = [slice(h * G // 2, (h + 1) * G // 2) for h in range(2)]
-
-        def gather(picked, window, pages):
-            nc.vector.tensor_copy(out=picked[:], in_=window[:].indirect(offsets[:, pages]))
+        def gather(picked, pool_tile, pages):
+            nc.vector.tensor_copy(out=picked[:], in_=pool_tile[:].indirect(offsets[:, pages]))
 
         def product(dst, rows, words, scales):
-            nc.tensor.matmul_mx(out=dst, lhsT=rows[0][:].bitcast(FP8X4), lhsT_scale=rows[1][:],
-                                rhs=words.bitcast(FP4X4), rhs_scale=scales, start=True, stop=True)
+            row_codes, row_scales = rows
+            nc.tensor.matmul_mx(
+                out=dst,
+                lhsT=row_codes[:].bitcast(FP8X4),
+                lhsT_scale=row_scales[:],
+                rhs=words.bitcast(FP4X4),
+                rhs_scale=scales,
+                start=True,
+                stop=True,
+            )
 
-        def by_page(dst, src, scale):
-            for g in range(scale.shape[1]):
+        def scale_by_page(dst, src, factors):
+            for g in range(factors.shape[1]):
                 columns = slice(g * PAGE, (g + 1) * PAGE)
-                nc.scalar.activation(out=dst[:, columns], in_=src[:, columns], func=ACT.Copy, scale=scale[:, g : g + 1])
+                nc.scalar.activation(out=dst[:, columns], in_=src[:, columns], func=ACT.Copy, scale=factors[:, g : g + 1])
 
-        all_pages = slice(0, G)
-        keys_pool = load_words("keys_pool", "keys_then_base", keys_words)
+        keys_pool = load_words("keys_pool", "keys_pool", keys_words)
+        offsets = sb.tile([P, I // LIST_ROWS], U16, name="offsets")
+        nc.sync.dma_start(offsets[:], offs)
         keys_plane = load_scales("keys_plane", keys_scales, nc.scalar)
-        query_raw = load_rows("query_raw", "query_then_gout", query)
-        dquery_raw = load_rows("dquery_raw", "dquery_raw", dquery)
-        warm = sb.tile([P, 2], F32, name="warm", tag="warm_then_vals")
-        nc.vector.memset(warm[:, 0:1], 0.0)
-        nc.scalar.activation(out=warm[:, 1:2], in_=warm[:, 0:1], func=ACT.Exp)
+        query_raw = load_rows("query_raw", "query_gout_base", query)
+        dquery_raw = load_rows("dquery_raw", "dquery_vals_rz", dquery)
         vals_plane = load_scales("vals_plane", vals_scales, nc.sync)
-        vals_pool = load_words("vals_pool", "warm_then_vals", vals_words)
-        help_col = narrow("help_col", 1)
+        help_col = floats("help_col", 1)
         nc.gpsimd.dma_start(out=help_col[:], in_=helpf)
         window = sb.tile([P, T], F32, name="window")
         nc.vector.memset(window[:], 0.0)
 
-        hc = narrow("hc", 4)
+        help_terms = floats("help_terms", 4)
         for column, (factor, shift) in enumerate(((0.5, 0.0), (0.5, 1.0), (-1.0 / 16, 0.0), (1.0 / 16, 0.0))):
-            nc.gpsimd.tensor_scalar(out=hc[:, column : column + 1], in0=help_col[:], scalar1=factor, scalar2=shift, op0=ALU.mult, op1=ALU.add)
+            nc.gpsimd.tensor_scalar(
+                out=help_terms[:, column : column + 1],
+                in0=help_col[:],
+                scalar1=factor,
+                scalar2=shift,
+                op0=ALU.mult,
+                op1=ALU.add,
+            )
+        fac_scale, fac_bias, kappa_scale, kappa_bias = (help_terms[:, j : j + 1] for j in range(4))
 
         query_bf = interleave("query_bf", "query_bf_then_keys_s1", query_raw)
         dquery_bf = interleave("dquery_bf", "dquery_bf", dquery_raw)
-        gout_raw = load_rows("gout_raw", "query_then_gout", gout)
+        gout_raw = load_rows("gout_raw", "query_gout_base", gout)
+        vals_pool = load_words("vals_pool", "dquery_vals_rz", vals_words)
         keys_w = sb.tile([P, I], U16, name="keys_w", align_bytes=64)
         keys_s = [sb.tile([P, HALF], U8, name="keys_s0", align_bytes=64)]
         gather(keys_w, keys_pool, all_pages)
-        base_sb = sb.tile([P, T], F32, name="base_sb", tag="keys_then_base")
-        nc.sync.dma_start(out=base_sb[:], in_=base)
         gather(keys_s[0], keys_plane, half_pages[0])
         query_q = quantize("query", query_bf)
         keys_s.append(sb.tile([P, HALF], U8, name="keys_s1", tag="query_bf_then_keys_s1", align_bytes=64))
@@ -128,103 +144,146 @@ def tile_attend_hvpagemates_s_kernel(tc, query, keys_words, keys_scales, helpf, 
         a = [psum.tile([P, I], F32, name="a%d" % h)[:, 0:HALF] for h in range(2)]
         for h in range(2):
             product(a[h], query_q, keys_w[:, halves[h]], keys_s[h][:])
-        a_sum = sb.tile([P, G], F32, name="a_sum")
+        a_sum = floats("a_sum", G)
         nc.vector.tensor_reduce(out=a_sum[:, half_pages[0]], in_=paged(a[0]), axis=AX.X, op=ALU.add)
         dquery_q = quantize("dquery", dquery_bf)
         ta = psum.tile([P, I], F32, name="ta")[:]
         for h in range(2):
             product(ta[:, halves[h]], dquery_q, keys_w[:, halves[h]], keys_s[h][:])
-        a_sb = wide("a_sb")
+        a_sb = floats("a_sb", I)
         nc.scalar.copy(out=a_sb[:, halves[0]], in_=a[0])
         nc.vector.tensor_reduce(out=a_sum[:, half_pages[1]], in_=paged(a[1]), axis=AX.X, op=ALU.add)
-        th = narrow("th")
+
+        th = floats("th", G)
         nc.scalar.activation(out=th[:], in_=a_sum[:], func=ACT.Tanh, scale=0.125)
-        fac = narrow("fac")
-        nc.scalar.activation(out=fac[:], in_=th[:], func=ACT.Identity, scale=hc[:, 0:1], bias=hc[:, 1:2])
-        ta_sb = wide("ta_sb")
+        fac = floats("fac", G)
+        nc.scalar.activation(out=fac[:], in_=th[:], func=ACT.Identity, scale=fac_scale, bias=fac_bias)
+        ta_sb = floats("ta_sb", I)
         nc.scalar.copy(out=ta_sb[:], in_=ta)
-        taf = wide("taf")
-        nc.gpsimd.tensor_tensor(out=paged(taf[:]), in0=paged(ta_sb[:]), in1=spread(fac[:]), op=ALU.mult)
-        th2 = narrow("th2")
-        nc.scalar.activation(out=th2[:], in_=th[:], func=ACT.Square)
-        kt = sb.tile([P, 2, G], F32, name="kt")
-        nc.scalar.activation(out=kt[:, 1, :], in_=th[:], func=ACT.Copy, scale=0.25)
-        nc.scalar.activation(out=kt[:, 0, :], in_=th2[:], func=ACT.Identity, scale=hc[:, 2:3], bias=hc[:, 3:4])
+        fac_ta = floats("fac_ta", I)
+        nc.gpsimd.tensor_tensor(out=paged(fac_ta[:]), in0=paged(ta_sb[:]), in1=spread(fac[:]), op=ALU.mult)
+        th_squared = floats("th_squared", G)
+        nc.scalar.activation(out=th_squared[:], in_=th[:], func=ACT.Square)
+        kappa_th4 = sb.tile([P, 2, G], F32, name="kappa_th4")
+        kappa = kappa_th4[:, 0, :]
+        nc.scalar.activation(out=kappa_th4[:, 1, :], in_=th[:], func=ACT.Copy, scale=0.25)
+        nc.scalar.activation(out=kappa, in_=th_squared[:], func=ACT.Identity, scale=kappa_scale, bias=kappa_bias)
         nc.scalar.copy(out=a_sb[:, halves[1]], in_=a[1])
         gout_bf = interleave("gout_bf", "gout_bf", gout_raw)
+        base_sb = sb.tile([P, T], F32, name="base_sb", tag="query_gout_base")
+        nc.sync.dma_start(out=base_sb[:], in_=base)
         vals_s = sb.tile([P, I], U8, name="vals_s", align_bytes=64)
         gather(vals_s, vals_plane, all_pages)
         ta_sum = sb.tile([P, G], F32, name="ta_sum", tag="ta_sum_then_vals_w", align_bytes=64)
         nc.vector.tensor_reduce(out=ta_sum[:], in_=paged(ta), axis=AX.X, op=ALU.add)
-        s = sb.tile([P, I], F32, name="s", tag="s_then_ka1")
+
+        s = sb.tile([P, I], F32, name="s", tag="s_then_k_a1")
         for h in range(2):
-            nc.vector.tensor_tensor(out=paged(s[:, halves[h]]), in0=paged(a[h]), in1=spread(fac[:, half_pages[h]]), op=ALU.mult)
-        uk = sb.tile([P, 2, G], F32, name="uk")
-        nc.vector.tensor_tensor(out=uk[:], in0=kt[:], in1=ta_sum[:].unsqueeze(1).to_broadcast([P, 2, G]), op=ALU.mult)
-        ua = sb.tile([P, I], F32, name="ua", tag="ua_then_nv")
-        nc.gpsimd.tensor_tensor(out=paged(ua[:]), in0=paged(a_sb[:]), in1=spread(uk[:, 0, :]), op=ALU.mult)
-        st = narrow("st", 8)
-        negmax, z, rz, cbar, tbar, cov = (st[:, j : j + 1] for j in range(6))
-        nc.vector.tensor_reduce(out=negmax, in_=s[:], axis=AX.X, op=ALU.max, negate=True)
-        e = wide("e")
-        nc.scalar.activation(out=e[:], in_=s[:], func=ACT.Exp, bias=negmax, accum_out=z)
+            nc.vector.tensor_tensor(
+                out=paged(s[:, halves[h]]), in0=paged(a[h]), in1=spread(fac[:, half_pages[h]]), op=ALU.mult
+            )
+        u_k = sb.tile([P, 2, G], F32, name="u_k")
+        nc.vector.tensor_tensor(
+            out=u_k[:], in0=kappa_th4[:], in1=ta_sum[:].unsqueeze(1).to_broadcast([P, 2, G]), op=ALU.mult
+        )
+        u, k = u_k[:, 0, :], u_k[:, 1, :]
+        u_a = sb.tile([P, I], F32, name="u_a", tag="u_a_then_nv")
+        nc.gpsimd.tensor_tensor(out=paged(u_a[:]), in0=paged(a_sb[:]), in1=spread(u), op=ALU.mult)
+        row_stats = floats("row_stats", 5)
+        nmax, z, cbar, tbar, cov = (row_stats[:, j : j + 1] for j in range(5))
+        nc.vector.tensor_reduce(out=nmax, in_=s[:], axis=AX.X, op=ALU.max, negate=True)
+        p = floats("p", I)
+        nc.scalar.activation(out=p[:], in_=s[:], func=ACT.Exp, bias=nmax, accum_out=z)
         gout_q = quantize("gout", gout_bf)
         vals_w = sb.tile([P, I], U16, name="vals_w", tag="ta_sum_then_vals_w", align_bytes=64)
         gather(vals_w, vals_pool, all_pages)
-        c = psum.tile([P, I], F32, name="c")[:]
-        product(c, gout_q, vals_w[:], vals_s[:])
+        c0 = psum.tile([P, I], F32, name="c0")[:]
+        product(c0, gout_q, vals_w[:], vals_s[:])
+        rz = sb.tile([P, 1], F32, name="rz", tag="dquery_vals_rz")[:]
         nc.vector.reciprocal(out=rz, in_=z)
-        prob = wide("prob")
-        nc.scalar.activation(out=prob[:], in_=e[:], func=ACT.Copy, scale=rz)
-        ts = wide("ts")
-        nc.vector.tensor_tensor(out=ts[:], in0=taf[:], in1=ua[:], op=ALU.add)
-        ka = [narrow("ka0", HALF), sb.tile([P, HALF], F32, name="ka1", tag="s_then_ka1")]
+        prob = floats("prob", I)
+        nc.scalar.activation(out=prob[:], in_=p[:], func=ACT.Copy, scale=rz)
+        ts = floats("ts", I)
+        nc.vector.tensor_tensor(out=ts[:], in0=fac_ta[:], in1=u_a[:], op=ALU.add)
+        k_a = [floats("k_a0", HALF), sb.tile([P, HALF], F32, name="k_a1", tag="s_then_k_a1")]
         for h in range(2):
-            by_page(ka[h], a_sb[:, halves[h]], uk[:, 1, half_pages[h]])
-        nfac512 = narrow("nfac512")
-        nc.scalar.activation(out=nfac512[:], in_=fac[:], func=ACT.Copy, scale=-512.0)
-        u512 = narrow("u512")
-        nc.scalar.activation(out=u512[:], in_=uk[:, 0, :], func=ACT.Copy, scale=512.0)
+            scale_by_page(k_a[h], a_sb[:, halves[h]], k[:, half_pages[h]])
+        nfac_gs = floats("nfac_gs", G)
+        nc.scalar.activation(out=nfac_gs[:], in_=fac[:], func=ACT.Copy, scale=-GS_FACTOR)
+        u_gs = floats("u_gs", G)
+        nc.scalar.activation(out=u_gs[:], in_=u, func=ACT.Copy, scale=GS_FACTOR)
 
-        pts = wide("pts")
-        nc.vector.scalar_tensor_tensor(out=pts[:], in0=ts[:], scalar=rz, in1=e[:], op0=ALU.mult, op1=ALU.mult, accum_out=tbar)
-        nv = sb.tile([P, I], F32, name="nv", tag="ua_then_nv")
+        prob_ts = floats("prob_ts", I)
+        nc.vector.scalar_tensor_tensor(
+            out=prob_ts[:], in0=ts[:], scalar=rz, in1=p[:], op0=ALU.mult, op1=ALU.mult, accum_out=tbar
+        )
+        nv = sb.tile([P, I], F32, name="nv", tag="u_a_then_nv")
         for h in range(2):
-            nc.gpsimd.tensor_tensor(out=nv[:, halves[h]], in0=ka[h][:], in1=ta_sb[:, halves[h]], op=ALU.subtract)
-        pc = wide("pc")
-        nc.vector.scalar_tensor_tensor(out=pc[:], in0=c, scalar=rz, in1=e[:], op0=ALU.mult, op1=ALU.mult, accum_out=cbar)
-        ds = wide("ds")
-        nc.vector.scalar_tensor_tensor(out=ds[:], in0=c, scalar=cbar, in1=prob[:], op0=ALU.subtract, op1=ALU.mult)
-        du = wide("du")
-        by_page(du, ds, u512)
-        r = sb.tile([P, I], F32, name="r", tag="r_then_terms1")
-        nc.vector.scalar_tensor_tensor(out=r[:], in0=ts[:], scalar=tbar, in1=ds[:], op0=ALU.subtract, op1=ALU.mult, accum_out=cov)
+            nc.gpsimd.tensor_tensor(out=nv[:, halves[h]], in0=k_a[h][:], in1=ta_sb[:, halves[h]], op=ALU.subtract)
+        prob_c0 = floats("prob_c0", I)
+        nc.vector.scalar_tensor_tensor(
+            out=prob_c0[:], in0=c0, scalar=rz, in1=p[:], op0=ALU.mult, op1=ALU.mult, accum_out=cbar
+        )
+        ds = floats("ds", I)
+        nc.vector.scalar_tensor_tensor(out=ds[:], in0=c0, scalar=cbar, in1=prob[:], op0=ALU.subtract, op1=ALU.mult)
+        gs_u = floats("gs_u", I)
+        scale_by_page(gs_u, ds, u_gs)
+        ds_ts = sb.tile([P, I], F32, name="ds_ts", tag="ds_ts_then_terms1")
+        nc.vector.scalar_tensor_tensor(
+            out=ds_ts[:], in0=ts[:], scalar=tbar, in1=ds[:], op0=ALU.subtract, op1=ALU.mult, accum_out=cov
+        )
+
         terms = [sb.tile([P, 2, HALF], F32, name="terms0")]
         nc.vector.tensor_tensor(out=terms[0][:, 1, :], in0=ds[:, halves[0]], in1=nv[:, halves[0]], op=ALU.mult)
-        ntds = wide("ntds")
+        ntds = floats("ntds", I)
         for h in range(2):
-            nc.vector.scalar_tensor_tensor(out=ntds[:, halves[h]], in0=prob[:, halves[h]], scalar=cov, in1=r[:, halves[h]], op0=ALU.mult, op1=ALU.subtract)
-        terms.append(sb.tile([P, 2, HALF], F32, name="terms1", tag="r_then_terms1"))
+            nc.vector.scalar_tensor_tensor(
+                out=ntds[:, halves[h]],
+                in0=prob[:, halves[h]],
+                scalar=cov,
+                in1=ds_ts[:, halves[h]],
+                op0=ALU.mult,
+                op1=ALU.subtract,
+            )
+        terms.append(sb.tile([P, 2, HALF], F32, name="terms1", tag="ds_ts_then_terms1"))
         nc.gpsimd.tensor_tensor(out=terms[1][:, 1, :], in0=ds[:, halves[1]], in1=nv[:, halves[1]], op=ALU.mult)
-        yf = wide("yf")
-        by_page(yf, ntds, nfac512)
+        gs_fac = floats("gs_fac", I)
+        scale_by_page(gs_fac, ntds, nfac_gs)
         for h in range(2):
             nc.vector.tensor_tensor(out=terms[h][:, 0, :], in0=a[h], in1=ntds[:, halves[h]], op=ALU.mult)
-        nx = narrow("nx")
+        nx = floats("nx", G)
         for h in range(2):
-            nc.vector.tensor_reduce(out=nx[:, half_pages[h]], in_=terms[h][:].rearrange("p s (g j) -> p g s j", j=PAGE), axis=AX.XY, op=ALU.add)
-        te = narrow("te")
+            nc.vector.tensor_reduce(
+                out=nx[:, half_pages[h]],
+                in_=terms[h][:].rearrange("p term (g j) -> p g term j", j=PAGE),
+                axis=AX.XY,
+                op=ALU.add,
+            )
+        gs_te = floats("gs_te", G)
         for h in range(2):
-            nc.vector.scalar_tensor_tensor(out=te[:, half_pages[h]], in0=nx[:, half_pages[h]], scalar=-512.0, in1=kt[:, 0, half_pages[h]], op0=ALU.mult, op1=ALU.mult)
-        y = wide("y")
+            nc.vector.scalar_tensor_tensor(
+                out=gs_te[:, half_pages[h]],
+                in0=nx[:, half_pages[h]],
+                scalar=-GS_FACTOR,
+                in1=kappa[:, half_pages[h]],
+                op0=ALU.mult,
+                op1=ALU.mult,
+            )
+
+        gs_u_te = floats("gs_u_te", I)
         for h in range(2):
-            nc.vector.tensor_tensor(out=paged(y[:, halves[h]]), in0=paged(du[:, halves[h]]), in1=spread(te[:, half_pages[h]]), op=ALU.add)
-        nc.vector.tensor_tensor(out=window[:].indirect(offsets[:]), in0=y[:], in1=yf[:], op=ALU.add)
+            nc.vector.tensor_tensor(
+                out=paged(gs_u_te[:, halves[h]]),
+                in0=paged(gs_u[:, halves[h]]),
+                in1=spread(gs_te[:, half_pages[h]]),
+                op=ALU.add,
+            )
+        nc.vector.tensor_tensor(out=window[:].indirect(offsets[:]), in0=gs_u_te[:], in1=gs_fac[:], op=ALU.add)
 
         start = 0
-        for index, width in enumerate(STORE_WIDTHS):
+        for piece, width in enumerate(STORE_WIDTHS):
             columns = slice(start, start + width)
-            result = sb.tile([P, width], F32, name="result%d" % index)
+            result = floats("result%d" % piece, width)
             nc.vector.tensor_tensor(out=result[:], in0=base_sb[:, columns], in1=window[:, columns], op=ALU.add)
             nc.sync.dma_start(out=out[:, columns], in_=result[:])
             start = start + width

from contextlib import ExitStack

import concourse.mybir as mybir

D, E, T, I, Q, G = 512, 512, 2048, 512, 128, 32
PAGE = I // G
FLOPS = 2 * Q * I * (2 * D + E)

F32 = mybir.dt.float32
BF16 = mybir.dt.bfloat16
I32 = mybir.dt.int32
U32 = mybir.dt.uint32
U16 = mybir.dt.uint16
U8 = mybir.dt.uint8
FP8X4 = mybir.dt.float8_e4m3fn_x4
FP4X4 = mybir.dt.float4_e2m1fn_x4
ALU = mybir.AluOpType
ACT = mybir.ActivationFunctionType
AX = mybir.AxisListType

P = 128
PACK = 4
QUADRANT = 32
SCALE_ROWS = 4
LIST_ROWS = 16
HALF = I // 2
GS_FACTOR = 512.0
STORE_WIDTHS = (256, 512, 512, 512, 256)


def tile_attend_hvpagemates_s_kernel(
    tc, query, keys_words, keys_scales, helpf, gout, vals_words, vals_scales, dquery, base, offs, out
):
    nc = tc.nc
    with ExitStack() as ctx:
        sb = ctx.enter_context(tc.tile_pool(name="sb", bufs=1))
        psum = ctx.enter_context(tc.psum_pool(name="psum", bufs=1))

        all_pages = slice(0, G)
        halves = [slice(h * HALF, (h + 1) * HALF) for h in range(2)]
        half_pages = [slice(h * G // 2, (h + 1) * G // 2) for h in range(2)]

        def floats(name, columns):
            return sb.tile([P, columns], F32, name=name)

        def paged(ap):
            return ap.rearrange("p (g j) -> p g j", j=PAGE)

        def spread(ap):
            return ap.unsqueeze(2).to_broadcast([P, ap.shape[1], PAGE])

        def load_words(name, tag, words):
            pool_words = sb.tile([P, T], U16, name=name, tag=tag)
            nc.sync.dma_start(out=pool_words[:].bitcast(I32), in_=words[0].bitcast(I32))
            return pool_words

        def load_scales(name, scales, queue):
            pool_scales = sb.tile([P, T], U8, name=name)
            nc.vector.memset(pool_scales[:].bitcast(I32), 0)
            for quadrant in range(P // QUADRANT):
                queue.dma_start(
                    out=pool_scales[QUADRANT * quadrant : QUADRANT * quadrant + SCALE_ROWS, :].bitcast(I32),
                    in_=scales[0, SCALE_ROWS * quadrant : SCALE_ROWS * (quadrant + 1), :].bitcast(I32),
                )
            return pool_scales

        def load_rows(name, tag, rows):
            raw = sb.tile([P, PACK, Q], F32, name=name, tag=tag)
            nc.sync.dma_start(out=raw[:], in_=rows.rearrange("(p r) q -> p r q", r=PACK))
            return raw

        def interleave(name, tag, raw):
            grouped = sb.tile([P, Q, PACK], BF16, name=name, tag=tag, align_bytes=64)
            nc.scalar.activation(
                out=grouped[:].rearrange("p (c i) r -> p c r i", i=4),
                in_=raw[:].rearrange("p r (c i) -> p c r i", i=4),
                func=ACT.Copy,
            )
            return grouped

        def quantize(name, grouped):
            codes = sb.tile([P, Q], U32, name=name + "_codes", align_bytes=64)
            scales = sb.tile([P, Q], U8, name=name + "_scales", align_bytes=64)
            nc.vector.quantize_mx(
                out=codes[:].bitcast(FP8X4), scales=scales[:], in_=grouped[:].rearrange("p q r -> p (q r)")
            )
            return codes, scales

        def gather(picked, pool_tile, pages):
            nc.vector.tensor_copy(out=picked[:], in_=pool_tile[:].indirect(offsets[:, pages]))

        def product(dst, rows, words, scales):
            row_codes, row_scales = rows
            nc.tensor.matmul_mx(
                out=dst,
                lhsT=row_codes[:].bitcast(FP8X4),
                lhsT_scale=row_scales[:],
                rhs=words.bitcast(FP4X4),
                rhs_scale=scales,
                start=True,
                stop=True,
            )

        def scale_by_page(dst, src, factors):
            for g in range(factors.shape[1]):
                columns = slice(g * PAGE, (g + 1) * PAGE)
                nc.scalar.activation(out=dst[:, columns], in_=src[:, columns], func=ACT.Copy, scale=factors[:, g : g + 1])

        keys_pool = load_words("keys_pool", "keys_pool", keys_words)
        offsets = sb.tile([P, I // LIST_ROWS], U16, name="offsets")
        nc.sync.dma_start(offsets[:], offs)
        keys_plane = load_scales("keys_plane", keys_scales, nc.scalar)
        query_raw = load_rows("query_raw", "query_gout_base", query)
        dquery_raw = load_rows("dquery_raw", "dquery_vals_rz", dquery)
        vals_plane = load_scales("vals_plane", vals_scales, nc.sync)
        help_col = floats("help_col", 1)
        nc.gpsimd.dma_start(out=help_col[:], in_=helpf)
        window = sb.tile([P, T], F32, name="window")
        nc.vector.memset(window[:], 0.0)

        help_terms = floats("help_terms", 4)
        for column, (factor, shift) in enumerate(((0.5, 0.0), (0.5, 1.0), (-1.0 / 16, 0.0), (1.0 / 16, 0.0))):
            nc.gpsimd.tensor_scalar(
                out=help_terms[:, column : column + 1],
                in0=help_col[:],
                scalar1=factor,
                scalar2=shift,
                op0=ALU.mult,
                op1=ALU.add,
            )
        fac_scale, fac_bias, kappa_scale, kappa_bias = (help_terms[:, j : j + 1] for j in range(4))

        query_bf = interleave("query_bf", "query_bf_then_keys_s1", query_raw)
        dquery_bf = interleave("dquery_bf", "dquery_bf", dquery_raw)
        gout_raw = load_rows("gout_raw", "query_gout_base", gout)
        vals_pool = load_words("vals_pool", "dquery_vals_rz", vals_words)
        keys_w = sb.tile([P, I], U16, name="keys_w", align_bytes=64)
        keys_s = [sb.tile([P, HALF], U8, name="keys_s0", align_bytes=64)]
        gather(keys_w, keys_pool, all_pages)
        gather(keys_s[0], keys_plane, half_pages[0])
        query_q = quantize("query", query_bf)
        keys_s.append(sb.tile([P, HALF], U8, name="keys_s1", tag="query_bf_then_keys_s1", align_bytes=64))
        gather(keys_s[1], keys_plane, half_pages[1])
        a = [psum.tile([P, I], F32, name="a%d" % h)[:, 0:HALF] for h in range(2)]
        for h in range(2):
            product(a[h], query_q, keys_w[:, halves[h]], keys_s[h][:])
        a_sum = floats("a_sum", G)
        nc.vector.tensor_reduce(out=a_sum[:, half_pages[0]], in_=paged(a[0]), axis=AX.X, op=ALU.add)
        dquery_q = quantize("dquery", dquery_bf)
        ta = psum.tile([P, I], F32, name="ta")[:]
        for h in range(2):
            product(ta[:, halves[h]], dquery_q, keys_w[:, halves[h]], keys_s[h][:])
        a_sb = floats("a_sb", I)
        nc.scalar.copy(out=a_sb[:, halves[0]], in_=a[0])
        nc.vector.tensor_reduce(out=a_sum[:, half_pages[1]], in_=paged(a[1]), axis=AX.X, op=ALU.add)

        th = floats("th", G)
        nc.scalar.activation(out=th[:], in_=a_sum[:], func=ACT.Tanh, scale=0.125)
        fac = floats("fac", G)
        nc.scalar.activation(out=fac[:], in_=th[:], func=ACT.Identity, scale=fac_scale, bias=fac_bias)
        ta_sb = floats("ta_sb", I)
        nc.scalar.copy(out=ta_sb[:], in_=ta)
        fac_ta = floats("fac_ta", I)
        nc.gpsimd.tensor_tensor(out=paged(fac_ta[:]), in0=paged(ta_sb[:]), in1=spread(fac[:]), op=ALU.mult)
        th_squared = floats("th_squared", G)
        nc.scalar.activation(out=th_squared[:], in_=th[:], func=ACT.Square)
        kappa_th4 = sb.tile([P, 2, G], F32, name="kappa_th4")
        kappa = kappa_th4[:, 0, :]
        nc.scalar.activation(out=kappa_th4[:, 1, :], in_=th[:], func=ACT.Copy, scale=0.25)
        nc.scalar.activation(out=kappa, in_=th_squared[:], func=ACT.Identity, scale=kappa_scale, bias=kappa_bias)
        nc.scalar.copy(out=a_sb[:, halves[1]], in_=a[1])
        gout_bf = interleave("gout_bf", "gout_bf", gout_raw)
        base_sb = sb.tile([P, T], F32, name="base_sb", tag="query_gout_base")
        nc.sync.dma_start(out=base_sb[:], in_=base)
        vals_s = sb.tile([P, I], U8, name="vals_s", align_bytes=64)
        gather(vals_s, vals_plane, all_pages)
        ta_sum = sb.tile([P, G], F32, name="ta_sum", tag="ta_sum_then_vals_w", align_bytes=64)
        nc.vector.tensor_reduce(out=ta_sum[:], in_=paged(ta), axis=AX.X, op=ALU.add)

        s = sb.tile([P, I], F32, name="s", tag="s_then_k_a1")
        for h in range(2):
            nc.vector.tensor_tensor(
                out=paged(s[:, halves[h]]), in0=paged(a[h]), in1=spread(fac[:, half_pages[h]]), op=ALU.mult
            )
        u_k = sb.tile([P, 2, G], F32, name="u_k")
        nc.vector.tensor_tensor(
            out=u_k[:], in0=kappa_th4[:], in1=ta_sum[:].unsqueeze(1).to_broadcast([P, 2, G]), op=ALU.mult
        )
        u, k = u_k[:, 0, :], u_k[:, 1, :]
        u_a = sb.tile([P, I], F32, name="u_a", tag="u_a_then_nv")
        nc.gpsimd.tensor_tensor(out=paged(u_a[:]), in0=paged(a_sb[:]), in1=spread(u), op=ALU.mult)
        row_stats = floats("row_stats", 5)
        nmax, z, cbar, tbar, cov = (row_stats[:, j : j + 1] for j in range(5))
        nc.vector.tensor_reduce(out=nmax, in_=s[:], axis=AX.X, op=ALU.max, negate=True)
        p = floats("p", I)
        nc.scalar.activation(out=p[:], in_=s[:], func=ACT.Exp, bias=nmax, accum_out=z)
        gout_q = quantize("gout", gout_bf)
        vals_w = sb.tile([P, I], U16, name="vals_w", tag="ta_sum_then_vals_w", align_bytes=64)
        gather(vals_w, vals_pool, all_pages)
        c0 = psum.tile([P, I], F32, name="c0")[:]
        product(c0, gout_q, vals_w[:], vals_s[:])
        rz = sb.tile([P, 1], F32, name="rz", tag="dquery_vals_rz")[:]
        nc.vector.reciprocal(out=rz, in_=z)
        prob = floats("prob", I)
        nc.scalar.activation(out=prob[:], in_=p[:], func=ACT.Copy, scale=rz)
        ts = floats("ts", I)
        nc.vector.tensor_tensor(out=ts[:], in0=fac_ta[:], in1=u_a[:], op=ALU.add)
        k_a = [floats("k_a0", HALF), sb.tile([P, HALF], F32, name="k_a1", tag="s_then_k_a1")]
        for h in range(2):
            scale_by_page(k_a[h], a_sb[:, halves[h]], k[:, half_pages[h]])
        nfac_gs = floats("nfac_gs", G)
        nc.scalar.activation(out=nfac_gs[:], in_=fac[:], func=ACT.Copy, scale=-GS_FACTOR)
        u_gs = floats("u_gs", G)
        nc.scalar.activation(out=u_gs[:], in_=u, func=ACT.Copy, scale=GS_FACTOR)

        prob_ts = floats("prob_ts", I)
        nc.vector.scalar_tensor_tensor(
            out=prob_ts[:], in0=ts[:], scalar=rz, in1=p[:], op0=ALU.mult, op1=ALU.mult, accum_out=tbar
        )
        nv = sb.tile([P, I], F32, name="nv", tag="u_a_then_nv")
        for h in range(2):
            nc.gpsimd.tensor_tensor(out=nv[:, halves[h]], in0=k_a[h][:], in1=ta_sb[:, halves[h]], op=ALU.subtract)
        prob_c0 = floats("prob_c0", I)
        nc.vector.scalar_tensor_tensor(
            out=prob_c0[:], in0=c0, scalar=rz, in1=p[:], op0=ALU.mult, op1=ALU.mult, accum_out=cbar
        )
        ds = floats("ds", I)
        nc.vector.scalar_tensor_tensor(out=ds[:], in0=c0, scalar=cbar, in1=prob[:], op0=ALU.subtract, op1=ALU.mult)
        gs_u = floats("gs_u", I)
        scale_by_page(gs_u, ds, u_gs)
        ds_ts = sb.tile([P, I], F32, name="ds_ts", tag="ds_ts_then_terms1")
        nc.vector.scalar_tensor_tensor(
            out=ds_ts[:], in0=ts[:], scalar=tbar, in1=ds[:], op0=ALU.subtract, op1=ALU.mult, accum_out=cov
        )

        terms = [sb.tile([P, 2, HALF], F32, name="terms0")]
        nc.vector.tensor_tensor(out=terms[0][:, 1, :], in0=ds[:, halves[0]], in1=nv[:, halves[0]], op=ALU.mult)
        ntds = floats("ntds", I)
        for h in range(2):
            nc.vector.scalar_tensor_tensor(
                out=ntds[:, halves[h]],
                in0=prob[:, halves[h]],
                scalar=cov,
                in1=ds_ts[:, halves[h]],
                op0=ALU.mult,
                op1=ALU.subtract,
            )
        terms.append(sb.tile([P, 2, HALF], F32, name="terms1", tag="ds_ts_then_terms1"))
        nc.gpsimd.tensor_tensor(out=terms[1][:, 1, :], in0=ds[:, halves[1]], in1=nv[:, halves[1]], op=ALU.mult)
        gs_fac = floats("gs_fac", I)
        scale_by_page(gs_fac, ntds, nfac_gs)
        for h in range(2):
            nc.vector.tensor_tensor(out=terms[h][:, 0, :], in0=a[h], in1=ntds[:, halves[h]], op=ALU.mult)
        nx = floats("nx", G)
        for h in range(2):
            nc.vector.tensor_reduce(
                out=nx[:, half_pages[h]],
                in_=terms[h][:].rearrange("p term (g j) -> p g term j", j=PAGE),
                axis=AX.XY,
                op=ALU.add,
            )
        gs_te = floats("gs_te", G)
        for h in range(2):
            nc.vector.scalar_tensor_tensor(
                out=gs_te[:, half_pages[h]],
                in0=nx[:, half_pages[h]],
                scalar=-GS_FACTOR,
                in1=kappa[:, half_pages[h]],
                op0=ALU.mult,
                op1=ALU.mult,
            )

        gs_u_te = floats("gs_u_te", I)
        for h in range(2):
            nc.vector.tensor_tensor(
                out=paged(gs_u_te[:, halves[h]]),
                in0=paged(gs_u[:, halves[h]]),
                in1=spread(gs_te[:, half_pages[h]]),
                op=ALU.add,
            )
        nc.vector.tensor_tensor(out=window[:].indirect(offsets[:]), in0=gs_u_te[:], in1=gs_fac[:], op=ALU.add)

        start = 0
        for piece, width in enumerate(STORE_WIDTHS):
            columns = slice(start, start + width)
            result = floats("result%d" % piece, width)
            nc.vector.tensor_tensor(out=result[:], in0=base_sb[:, columns], in1=window[:, columns], op=ALU.add)
            nc.sync.dma_start(out=out[:, columns], in_=result[:])
            start = start + width
